import numpy as np
import ml_dtypes


def mxq(x, axis, fmt="e4m3"):
    dtype, down = {"e4m3": (ml_dtypes.float8_e4m3fn, 7), "e5m2": (ml_dtypes.float8_e5m2, 14)}[fmt]
    v = np.moveaxis(np.asarray(x, np.float32).astype(ml_dtypes.bfloat16).astype(np.float64), axis, -1)
    blocks = v.reshape(v.shape[:-1] + (-1, 32))
    amax = np.abs(blocks).max(-1, keepdims=True)
    byte = np.maximum(np.where(amax > 0, np.frexp(amax)[1] - 1 + 127, 0) - down, 1)
    scale = np.exp2(byte - 127.0)
    codes = (blocks / scale).astype(np.float32).astype(dtype).astype(np.float64)
    return np.moveaxis((codes * scale).reshape(v.shape), -1, axis)


WIDE = False


def mx_kscale(k):
    if not WIDE:
        return np.ones(k)
    levels = np.array([10, -10, 5, -5, 0])
    if k % 512:
        return np.exp2(np.random.permutation(np.resize(levels, k // 32))).repeat(32)
    a = np.empty((k // 512, 16))
    for p in range(k // 512):
        a[p, :8] = np.random.permutation(np.resize(levels, 8))
        for g in range(8):
            far = levels[np.abs(levels - a[p, g]) >= 10]
            a[p, g + 8] = far[np.random.randint(len(far))]
    return np.exp2(a.ravel()).repeat(32)


def f64(x):
    return np.asarray(x).astype(np.float64)


def striped(idx):
    return np.tile(np.asarray(idx).reshape(-1, 16).T, (8, 1)).astype(np.uint16)


def unstriped(offs):
    return offs[:16].T.reshape(-1).astype(np.int64)


E2M1 = np.array([0.0, 0.5, 1.0, 1.5, 2.0, 3.0, 4.0, 6.0, -0.0, -0.5, -1.0, -1.5, -2.0, -3.0, -4.0, -6.0])


def pack_weight(w, fmt):
    k, n = w.shape
    w = f64(np.asarray(w, np.float32).astype(ml_dtypes.bfloat16)).reshape(k // 32, 32, n)
    amax = np.abs(w).max(1)
    if fmt == "e4m3":
        byte = np.frexp(amax)[1] - 1 + 127 - 7
    else:
        mant, ex = np.frexp(amax / 6.0)
        byte = np.where(mant > 0.5, ex, ex - 1) + 127
    byte = np.clip(np.where(amax > 0, byte, 1), 1, 254)
    scaled = (w * np.exp2(127.0 - byte)[:, None, :]).reshape(k, n).astype(np.float32)
    by_word = np.ascontiguousarray(scaled.reshape(k // 512, 128, 4, n).transpose(0, 1, 3, 2))
    if fmt == "e4m3":
        words = by_word.astype(ml_dtypes.float8_e4m3fn).view(np.uint8)
    else:
        c = by_word.astype(ml_dtypes.float4_e2m1fn).view(np.uint8) & 0xF
        words = (c[..., 0::2] | (c[..., 1::2] << 4)).reshape(k // 512, 128, 2 * n)
    return np.ascontiguousarray(words), np.ascontiguousarray(byte.astype(np.uint8).reshape(k // 512, 16, n))


def unpack_weight(words, scales, fmt):
    g, _, n = scales.shape
    words = np.ascontiguousarray(words).reshape(g, 128, n, -1)
    if fmt == "e4m3":
        vals = words.view(ml_dtypes.float8_e4m3fn).astype(np.float64)
    else:
        nib = np.empty((g, 128, n, 4), np.uint8)
        nib[..., 0::2] = words & 0xF
        nib[..., 1::2] = words >> 4
        vals = E2M1[nib]
    vals = vals * np.repeat(np.exp2(scales.astype(np.float64) - 127.0), 8, axis=1)[..., None]
    return vals.transpose(0, 1, 3, 2).reshape(g * 512, n)


def bf(x):
    return np.asarray(x, np.float32).astype(ml_dtypes.bfloat16)


def planes(Y):
    r, m = Y.shape
    b = f64(bf(Y)).reshape(r // 32, 32, m)
    amax = np.abs(b).max(1)
    byte = np.clip(np.where(amax > 0, np.frexp(amax)[1] - 1 + 127 - 7, 1), 1, 254)
    codes = (b * np.exp2(127.0 - byte)[:, None, :]).reshape(r, m).astype(np.float32).astype(ml_dtypes.float8_e4m3fn).view(np.uint8)
    words = codes.reshape(r // 512, 128, 4, m).transpose(0, 1, 3, 2)
    return np.ascontiguousarray(words), np.ascontiguousarray(byte.astype(np.uint8).reshape(r // 512, 16, m))


D, T, I, Q, E, G = 512, 2048, 512, 256, 512, 64


def setup_inputs():
    n = np.random.standard_normal
    idx = np.random.permutation(T)[:I]
    fd = mx_kscale(D)
    fi = mx_kscale(I)
    ti = np.ones(T)
    ti[idx] = fi
    keysp = pack_weight(n((D, T)) / fd[:, None], "e2m1")
    return {
        "query": (n((D, Q)) * 0.7 / np.sqrt(D) * fd[:, None]).astype(np.float32),
        "query2": (n((D, Q)) * 0.7 / np.sqrt(D) * fd[:, None]).astype(np.float32),
        "keys_words": keysp[0],
        "keys_scales": keysp[1],
        "xmark": np.tile(np.random.uniform(-1.0, 1.0, T), (128, 1)).astype(np.float32),
        "ymark": np.tile(np.random.uniform(-1.0, 1.0, T), (128, 1)).astype(np.float32),
        "lam": (np.random.uniform(0.5, 1.2, (Q, 1))).astype(np.float32),
        "os": (np.random.uniform(4.0, 16.0, (1, I)) * fi).astype(np.float32),
        "vals": (n((E, T)) / ti).astype(np.float32),
        "before": (n((E, Q))).astype(np.float32),
        "hold": (np.random.uniform(0.1, 0.6, (1, Q))).astype(np.float32),
        "offs": striped(idx),
    }


def reference(query, query2, keys_words, keys_scales, xmark, ymark, lam, os, vals, before, hold, offs):
    idx = unstriped(offs)
    keysu = unpack_weight(keys_words, keys_scales, "e2m1")
    queryq = mxq(f64(query), 0, "e4m3")
    keysidxg = keysu[:, idx]
    a = queryq.T @ keysidxg
    query2q = mxq(f64(query2), 0, "e4m3")
    b = query2q.T @ keysidxg
    dx = a - f64(xmark)[:1][:, idx]
    dy = b - f64(ymark)[:1][:, idx]
    s = (np.square(dx) + np.square(dy)) * f64(lam) * (-1.0)
    p = np.exp(s)
    pg = p.reshape(Q, G, I // G).sum(axis=2)
    z0 = np.sum(pg, axis=1, keepdims=True)
    k0 = 1.0 / (z0 - pg)
    kr = np.repeat(k0, I // G, axis=1)
    w = p * kr
    wo1 = w * f64(os)
    wt1 = wo1.T
    vt1 = f64(vals)[:, idx].T
    vt1q = mxq(vt1, 0, "e4m3")
    wt1q = mxq(wt1, 0, "e4m3")
    o = vt1q.T @ wt1q
    y = f64(before) * f64(hold) + o * (1.0 - f64(hold))
    words, scales = planes(y)
    return y, words, scales

from contextlib import ExitStack

import concourse.mybir as mybir
from concourse.masks import make_identity

D, T, I, Q, E = 512, 2048, 512, 256, 512
RUN = 8
G = I // RUN
P = 128
PACK = 4
HALVES = Q // P
LIVE = P - 1
FLOPS = 2 * (2 * D * Q * I) + 2 * I * E * Q

F32 = mybir.dt.float32
BF16 = mybir.dt.bfloat16
I32 = mybir.dt.int32
U32 = mybir.dt.uint32
U16 = mybir.dt.uint16
U8 = mybir.dt.uint8
FP8X4 = mybir.dt.float8_e4m3fn_x4
FP4X4 = mybir.dt.float4_e2m1fn_x4
ALU = mybir.AluOpType
ACT = mybir.ActivationFunctionType
AXIS = mybir.AxisListType


def tile_attend_maplace_outside_blend_pl_kernel(
    tc, query, query2, keys_words, keys_scales, xmark, ymark, lam, slot_factor, vals, before, hold, offs, out_0, out_1, out_2
):
    nc = tc.nc
    with ExitStack() as ctx:
        sb = ctx.enter_context(tc.tile_pool(name="sb", bufs=1))
        ps = ctx.enter_context(tc.psum_pool(name="ps", bufs=1))

        def tile(name, shape, dtype, over=None):
            return sb.tile(shape, dtype, name=name, tag=over or name, align_bytes=64)

        def bank(name, number):
            return ps.tile([P, 512], F32, name=name, tag="bank%d" % number)

        offsets = sb.tile([P, I // 16], U16, name="offsets")
        key_pool = tile("key_pool", [P, T], U16)
        scale_pool = tile("scale_pool", [P, T], U8)
        x_pool = tile("x_pool", [P, T], F32)
        y_pool = tile("y_pool", [P, T], F32)
        q_raw = [tile("q_raw%d" % a, [P, PACK, Q], F32) for a in range(2)]
        val_pool = [tile("val_pool0", [P, T], F32)]
        lam_col = tile("lam_col", [P, HALVES], F32)
        os_col = tile("os_col", [P, PACK], F32)
        hold_col = tile("hold_col", [P, HALVES], F32)
        ident = tile("ident", [P, P], F32)

        nc.vector.memset(scale_pool[:].bitcast(I32), 0)
        nc.vector.memset(x_pool[0:LIVE, :], 0.0)
        nc.vector.memset(y_pool[0:LIVE, :], 0.0)
        make_identity(nc, ident[:])

        nc.sync.dma_start(offsets[:], offs)
        nc.sync.dma_start(x_pool[LIVE:P, :], xmark[0:1, :])
        nc.sync.dma_start(y_pool[LIVE:P, :], ymark[0:1, :])
        nc.sync.dma_start(key_pool[:].bitcast(I32), keys_words[0].bitcast(I32))
        for raw, source in zip(q_raw, (query, query2)):
            nc.sync.dma_start(raw[:], source.rearrange("(p j) q -> p j q", j=PACK))
        for quad in range(4):
            nc.scalar.dma_start(
                scale_pool[32 * quad : 32 * quad + 4, :].bitcast(I32),
                keys_scales[0, 4 * quad : 4 * quad + 4, :].bitcast(I32),
            )
        vals_dealt = vals.rearrange("(p j) t -> j p t", j=PACK)
        nc.sync.dma_start(val_pool[0][:], vals_dealt[0])
        nc.gpsimd.dma_start(os_col[:], slot_factor.rearrange("o (p j) -> p (o j)", j=PACK))
        nc.gpsimd.dma_start(hold_col[:], hold.rearrange("o (p c) -> p (o c)", c=HALVES))
        with nc.allow_non_contiguous_dma(reason="one factor a query row, one row a partition"):
            nc.gpsimd.dma_start(lam_col[:], lam.rearrange("(c p) o -> p (c o)", p=P))

        key_words = tile("key_words", [P, I], U16)
        key_scales = tile("key_scales", [P, I], U8)
        nc.vector.tensor_copy(key_words[:], key_pool[:].indirect(offsets[:]))
        nc.vector.tensor_copy(key_scales[:], scale_pool[:].indirect(offsets[:]))

        x_row = tile("x_row", [P, I], F32)
        y_row = tile("y_row", [P, I], F32)
        nc.scalar.activation(x_row[:], x_pool[:].indirect(offsets[:]), ACT.Copy)
        nc.scalar.activation(y_row[:], y_pool[:].indirect(offsets[:]), ACT.Copy)
        for j, over in ((1, "key_pool"), (2, "x_pool"), (3, "y_pool")):
            val_pool.append(tile("val_pool%d" % j, [P, T], F32, over))
            nc.sync.dma_start(val_pool[j][:], vals_dealt[j])
        before_sb = tile("before_sb", [P, PACK, Q], F32, "scale_pool")
        nc.sync.dma_start(before_sb[:], before.rearrange("(p j) q -> p j q", j=PACK))
        marks = tile("marks", [P, 2, 4], F32)
        for a, row in enumerate((x_row, y_row)):
            marks_ps = bank("marks_ps%d" % a, 6 + a)
            for m in range(4):
                cols = slice(m * P, (m + 1) * P)
                nc.tensor.transpose(marks_ps[:, cols], row[:, cols], ident[:])
            nc.scalar.copy(marks[:, a], marks_ps[:, LIVE : I : P])

        q_grouped = tile("q_grouped", [P, HALVES, 2, P, PACK], BF16)
        q_codes = tile("q_codes", [P, HALVES, 2 * P], U32)
        q_scales = tile("q_scales", [P, HALVES, 2 * P], U8)
        for c in range(HALVES):
            cols = slice(c * P, (c + 1) * P)
            nc.gpsimd.tensor_copy(q_grouped[:, c, 0], q_raw[0][:, :, cols].rearrange("p j q -> p q j"))
        for c in range(HALVES):
            cols = slice(c * P, (c + 1) * P)
            nc.vector.tensor_copy(
                q_grouped[:, c, 1].rearrange("p (n i) j -> p n j i", i=4),
                q_raw[1][:, :, cols].rearrange("p j (n i) -> p n j i", i=4),
            )
        for c in range(HALVES):
            nc.vector.quantize_mx(
                out=q_codes[:, c].bitcast(FP8X4),
                scales=q_scales[:, c],
                in_=q_grouped[:, c].rearrange("p a q j -> p (a q j)"),
            )

        os_ps = bank("os_ps", 4)
        for j in range(PACK):
            nc.tensor.transpose(os_ps[:, j * P : (j + 1) * P], os_col[:, j : j + 1].to_broadcast([P, P]), ident[:])
        os_row = tile("os_row", [P, P, PACK], F32)
        nc.scalar.copy(os_row[:], os_ps[:].rearrange("x (j p) -> x p j", j=PACK))
        hold_ps = bank("hold_ps", 5)
        for c in range(HALVES):
            nc.tensor.transpose(hold_ps[:, c * P : (c + 1) * P], hold_col[:, c : c + 1].to_broadcast([P, P]), ident[:])
        hold_view = hold_ps[:, 0:Q].rearrange("x (c p) -> x p c", c=HALVES)
        hold_row = tile("hold_row", [P, P, HALVES], F32)
        rest_row = tile("rest_row", [P, P, HALVES], F32)
        nc.scalar.copy(hold_row[:], hold_view)
        nc.scalar.activation(rest_row[:], hold_view, ACT.Copy, bias=1.0, scale=-1.0)
        minus_lam = tile("minus_lam", [P, HALVES], F32)
        nc.gpsimd.tensor_scalar(minus_lam[:], lam_col[:], -1.0, 0.0, ALU.mult, ALU.add)

        squares = tile("squares", [P, HALVES, 4, 2, P], F32)
        p_sb = tile("p_sb", [P, HALVES, I], F32)
        po_sb = tile("po_sb", [P, HALVES, I], F32)
        z0 = tile("z0", [P, HALVES], F32)
        points = {}
        for c in range(HALVES):
            for pair in range(2):
                points[c, pair] = bank("points%d%d" % (c, pair), 2 * c + pair)
                for n in range(2):
                    m = 2 * pair + n
                    nc.tensor.matmul_mx(
                        out=points[c, pair][:, n * 2 * P : (n + 1) * 2 * P],
                        lhsT=key_words[:, m * P : (m + 1) * P].bitcast(FP4X4),
                        lhsT_scale=key_scales[:, m * P : (m + 1) * P],
                        rhs=q_codes[:, c].bitcast(FP8X4),
                        rhs_scale=q_scales[:, c],
                        start=True,
                        stop=True,
                    )
        for c in range(HALVES):
            dist_ps = bank("dist%d" % c, 4 + c)
            for m in range(4):
                for a in range(2):
                    at = ((m % 2) * 2 + a) * P
                    nc.scalar.activation(
                        squares[:, c, m, a], points[c, m // 2][:, at : at + P], ACT.Square,
                        bias=marks[:, a, m : m + 1], scale=-1.0,
                    )
                    nc.tensor.matmul(
                        dist_ps[:, m * P : (m + 1) * P], squares[:, c, m, a], ident[:],
                        start=(a == 0), stop=(a == 1), is_transpose=True,
                    )
            nc.scalar.activation(
                p_sb[:, c], dist_ps[:], ACT.Exp, scale=minus_lam[:, c : c + 1], accum_out=z0[:, c : c + 1]
            )
            nc.gpsimd.tensor_tensor(po_sb[:, c], p_sb[:, c], os_row[:].rearrange("x p j -> x (p j)"), ALU.mult)

        val_codes = tile("val_codes", [P, PACK, P], U32)
        val_scales = tile("val_scales", [P, PACK, P], U8)

        def values(j, engine):
            picked = tile("picked%d" % j, [P, I], BF16)
            if engine == "vector":
                nc.vector.tensor_copy(picked[:], val_pool[j][:].indirect(offsets[:]))
            else:
                nc.scalar.activation(picked[:], val_pool[j][:].indirect(offsets[:]), ACT.Copy)
            turned = bank("val_turned%d" % j, 6 + (j + 1) % 2)
            words = picked[:].bitcast(F32)
            for u in range(2):
                nc.tensor.transpose(turned[:, u * P : (u + 1) * P], words[:, u : 2 * P : 2], ident[:])
            grouped = tile("val_grouped%d" % j, [P, P * PACK], BF16)
            nc.scalar.copy(
                grouped[:].bitcast(F32).rearrange("s (m u) -> s m u", u=2),
                turned[:, 0 : 2 * P].rearrange("s (u m) -> s m u", u=2),
            )
            nc.vector.quantize_mx(out=val_codes[:, j].bitcast(FP8X4), scales=val_scales[:, j], in_=grouped[:])

        values(0, "vector")
        values(1, "vector")

        pg = tile("pg", [P, HALVES, G], F32)
        rest = tile("rest", [P, HALVES, G], F32)
        k0 = tile("k0", [P, HALVES, G], F32)
        w_codes = tile("w_codes", [P, Q], U32)
        w_scales = tile("w_scales", [P, Q], U8)
        for c in range(HALVES):
            nc.vector.tensor_reduce(pg[:, c], p_sb[:, c].rearrange("q (g u) -> q g u", u=RUN), AXIS.X, ALU.add)
            nc.vector.tensor_scalar(rest[:, c], pg[:, c], -1.0, z0[:, c : c + 1], ALU.mult, ALU.add)
            nc.vector.reciprocal(k0[:, c], rest[:, c])
            w_rows = tile("w_rows%d" % c, [P, I], BF16)
            nc.vector.tensor_tensor(
                w_rows[:].rearrange("q (g u) -> q g u", u=RUN),
                po_sb[:, c].rearrange("q (g u) -> q g u", u=RUN),
                k0[:, c].unsqueeze(2).to_broadcast([P, G, RUN]),
                ALU.mult,
            )
            turned = bank("w_turned%d" % c, 4 + c)
            words = w_rows[:].bitcast(F32)
            for u in range(2):
                nc.tensor.transpose(turned[:, u * P : (u + 1) * P], words[:, u : 2 * P : 2], ident[:])
            grouped = tile("w_grouped%d" % c, [P, P * PACK], BF16)
            nc.scalar.copy(
                grouped[:].bitcast(F32).rearrange("s (m u) -> s m u", u=2),
                turned[:, 0 : 2 * P].rearrange("s (u m) -> s m u", u=2),
            )
            cols = slice(c * P, (c + 1) * P)
            nc.vector.quantize_mx(out=w_codes[:, cols].bitcast(FP8X4), scales=w_scales[:, cols], in_=grouped[:])

        values(2, "scalar")
        values(3, "scalar")

        kept = tile("kept", [P, PACK, Q], F32)
        added = tile("added", [P, PACK, Q], F32)
        y = tile("y", [P, PACK, Q], F32)
        out_dealt = out_0.rearrange("(p j) q -> p j q", j=PACK)
        for j in range(PACK):
            nc.gpsimd.tensor_tensor(kept[:, j], before_sb[:, j], hold_row[:].rearrange("x p c -> x (p c)"), ALU.mult)
        for j in range(PACK):
            o_ps = bank("o%d" % j, j)
            nc.tensor.matmul_mx(
                out=o_ps[:, 0:Q],
                lhsT=val_codes[:, j].bitcast(FP8X4),
                lhsT_scale=val_scales[:, j],
                rhs=w_codes[:].bitcast(FP8X4),
                rhs_scale=w_scales[:],
                start=True,
                stop=True,
            )
            nc.vector.tensor_tensor(added[:, j], o_ps[:, 0:Q], rest_row[:].rearrange("x p c -> x (p c)"), ALU.mult)
        for j in range(PACK):
            nc.vector.tensor_tensor(y[:, j], added[:, j], kept[:, j], ALU.add)
            nc.sync.dma_start(out_dealt[:, j], y[:, j])

        y_grouped = tile("y_grouped", [P, Q, PACK], BF16)
        y_codes = tile("y_codes", [P, Q], U32)
        y_scales = tile("y_scales", [P, Q], U8)
        nc.vector.tensor_copy(
            y_grouped[:].rearrange("p (n i) j -> p n j i", i=4), y[:].rearrange("p j (n i) -> p n j i", i=4)
        )
        nc.vector.quantize_mx(
            out=y_codes[:].bitcast(FP8X4), scales=y_scales[:], in_=y_grouped[:].rearrange("p q j -> p (q j)")
        )
        nc.sync.dma_start(out_1[0].rearrange("p c r -> p (c r)").bitcast(I32), y_codes[:].bitcast(I32))
        for quad in range(4):
            queue = nc.scalar if quad % 2 else nc.sync
            queue.dma_start(
                out_2[0, 4 * quad : 4 * quad + 4, :].bitcast(I32),
                y_scales[32 * quad : 32 * quad + 4, :].bitcast(I32),
            )
